import numpy as np
import ml_dtypes


def mxq(x, axis, fmt="e4m3"):
    dtype, down = {"e4m3": (ml_dtypes.float8_e4m3fn, 7), "e5m2": (ml_dtypes.float8_e5m2, 14)}[fmt]
    v = np.moveaxis(np.asarray(x, np.float32).astype(ml_dtypes.bfloat16).astype(np.float64), axis, -1)
    blocks = v.reshape(v.shape[:-1] + (-1, 32))
    amax = np.abs(blocks).max(-1, keepdims=True)
    byte = np.maximum(np.where(amax > 0, np.frexp(amax)[1] - 1 + 127, 0) - down, 1)
    scale = np.exp2(byte - 127.0)
    codes = (blocks / scale).astype(np.float32).astype(dtype).astype(np.float64)
    return np.moveaxis((codes * scale).reshape(v.shape), -1, axis)


WIDE = False


def mx_kscale(k):
    if not WIDE:
        return np.ones(k)
    levels = np.array([10, -10, 5, -5, 0])
    if k % 512:
        return np.exp2(np.random.permutation(np.resize(levels, k // 32))).repeat(32)
    a = np.empty((k // 512, 16))
    for p in range(k // 512):
        a[p, :8] = np.random.permutation(np.resize(levels, 8))
        for g in range(8):
            far = levels[np.abs(levels - a[p, g]) >= 10]
            a[p, g + 8] = far[np.random.randint(len(far))]
    return np.exp2(a.ravel()).repeat(32)


BF16 = ml_dtypes.bfloat16


def bf(x):
    return np.asarray(x, np.float32).astype(BF16)


def f64(x):
    return np.asarray(x).astype(np.float64)

E4M3FN = np.array([(-1.0 if i & 128 else 1.0) * ((1.0 + (i & 7) / 8.0) * 2.0 ** (((i >> 3) & 15) - 7) if i & 120 else (i & 7) * 2.0 ** -9) for i in range(256)])


def e4m3fn_bytes(y):
    return np.clip(np.asarray(y, np.float64), -448.0, 448.0).astype(np.float32).astype(ml_dtypes.float8_e4m3fn).view(np.uint8)


def e4m3fn_values(b):
    return E4M3FN[b]


T, D, F = 768, 1024, 1536


def setup_inputs():
    s, t = mx_kscale(D), mx_kscale(F)
    wg = 1.5 * np.random.standard_normal((D, F)) / np.sqrt(D) / s[:, None]
    wd = 2.0 * np.random.standard_normal((F, D)) / np.sqrt(F) / t[:, None]
    wg_scale = (np.max(np.abs(wg), axis=1, keepdims=True) / 448.0).astype(np.float32)
    wd_scale = (np.max(np.abs(wd), axis=1, keepdims=True) / 448.0).astype(np.float32)
    return {"x": bf(np.random.standard_normal((T, D)) * s),
            "wg_bytes": e4m3fn_bytes(wg / f64(wg_scale)),
            "wg_scale": wg_scale,
            "bg": bf(0.5 * np.random.standard_normal(F)),
            "wu": bf(np.random.standard_normal((D, F)) / np.sqrt(D) / s[:, None] * t),
            "wd_bytes": e4m3fn_bytes(wd / f64(wd_scale)),
            "wd_scale": wd_scale,
            "routed": bf(np.random.standard_normal((T, D)))}


def reference(x, wg_bytes, wg_scale, bg, wu, wd_bytes, wd_scale, routed):
    wg = e4m3fn_values(wg_bytes) * np.repeat(f64(wg_scale), F, axis=1)
    wd = e4m3fn_values(wd_bytes) * np.repeat(f64(wd_scale), D, axis=1)
    xq = mxq(f64(x), 1, "e4m3")
    z = (xq @ mxq(wg, 0, "e4m3")) + f64(bg)
    u = xq @ mxq(f64(wu), 0, "e4m3")
    h = u * (1.0 / (1.0 + np.exp(-z)))
    y = mxq(h, 1, "e4m3") @ mxq(wd, 0, "e4m3")
    return f64(routed) + y

@@ -1,0 +1,294 @@
+from contextlib import ExitStack
+
+import concourse.mybir as mybir
+from concourse.masks import make_identity
+
+T, D, F = 768, 1024, 1536
+FLOPS = 2 * T * D * F * 2 + 2 * T * F * D
+
+P = 128
+J = 4
+KP = P * J
+W = 512
+NC = D // KP
+NG = F // KP
+NH = D // W
+TG = 256
+NTG = T // TG
+
+F32 = mybir.dt.float32
+BF16 = mybir.dt.bfloat16
+U32 = mybir.dt.uint32
+U8 = mybir.dt.uint8
+FP8 = mybir.dt.float8_e4m3fn
+FP8X4 = mybir.dt.float8_e4m3fn_x4
+ACT = mybir.ActivationFunctionType
+ALU = mybir.AluOpType
+
+
+def tile_shared_expert_sigmoid_glu_d5_kernel(tc, x, wg_bytes, wg_scale, bg, wu, wd_bytes, wd_scale, routed, out):
+    nc = tc.nc
+    with ExitStack() as ctx:
+        keep = ctx.enter_context(tc.tile_pool(name="keep", bufs=1))
+        stage = ctx.enter_context(tc.tile_pool(name="stage", bufs=4))
+        psum = ctx.enter_context(tc.psum_pool(name="psum", bufs=8))
+        ctx.enter_context(tc.manual_schedule())
+
+        wgs = keep.tile([P, NC, 8], F32, name="wgs")
+        nc.scalar.dma_start(out=wgs[:, :, 0:J], in_=wg_scale.rearrange("(c p t) o -> p c (t o)", p=P, t=J))
+        wgb = {}
+        wur = {}
+        xs = {}
+        wdb = {}
+
+        def load_wg(c, lo, n, key):
+            t_ = keep.tile([P, J, n], U8, name="wgb_%d_%d" % (c, lo))
+            nc.sync.dma_start(out=t_[:], in_=wg_bytes[c * KP:(c + 1) * KP, lo:lo + n].rearrange("(p j) n -> p j n", j=J))
+            for g in key:
+                wgb[c, g] = t_[:, :, g * W - lo:(g + 1) * W - lo]
+
+        def load_wu(c, lo, n, key):
+            t_ = keep.tile([P, J, n], BF16, name="wur_%d_%d" % (c, lo))
+            nc.sync.dma_start(out=t_[:], in_=wu[c * KP:(c + 1) * KP, lo:lo + n].rearrange("(p j) n -> p j n", j=J))
+            for g in key:
+                wur[c, g] = t_[:, :, g * W - lo:(g + 1) * W - lo]
+
+        def load_x(b):
+            t_ = keep.tile([P, D], BF16, name="x_%d" % b)
+            nc.sync.dma_start(out=t_[:], in_=x[b * P:(b + 1) * P, :])
+            xs[b] = t_
+
+        load_wg(0, 0, W, (0,))
+        load_wu(0, 0, W, (0,))
+        load_x(0)
+        load_x(1)
+        load_wg(1, 0, W, (0,))
+        load_wu(1, 0, W, (0,))
+        for b in range(2, 6):
+            load_x(b)
+        for c in range(NC):
+            load_wg(c, W, 2 * W, (1, 2))
+            load_wu(c, W, 2 * W, (1, 2))
+        bias = keep.tile([P, NG, J], BF16, name="bias")
+        nc.scalar.dma_start(out=bias[:], in_=bg.rearrange("(g p t) -> p g t", p=P, t=J))
+        wds = keep.tile([P, NG, 8], F32, name="wds")
+        nc.scalar.dma_start(out=wds[:, :, 0:J], in_=wd_scale.rearrange("(g p t) o -> p g (t o)", p=P, t=J))
+        for g in range(NG):
+            wdt = keep.tile([P, J, D], U8, name="wdb_%d" % g)
+            nc.sync.dma_start(out=wdt[:], in_=wd_bytes[g * KP:(g + 1) * KP, :].rearrange("(p j) n -> p j n", j=J))
+            wdb[g] = wdt
+        rt = keep.tile([P, T // P, D], BF16, name="rt")
+        for q in range(2):
+            nc.sync.dma_start(out=rt[:, 3 * q:3 * q + 3, :], in_=routed[3 * P * q:3 * P * (q + 1), :].rearrange("(b p) n -> p b n", p=P))
+
+        warm = keep.tile([P, 1], F32, name="warm")
+        nc.vector.memset(warm[:], 0.0)
+        nc.scalar.activation(out=warm[:], in_=warm[:], func=ACT.Sigmoid)
+        ident = keep.tile([P, P], F32, name="ident")
+        make_identity(nc, ident[:])
+
+        wide = {}
+        grp = {}
+        codes = {}
+        scales = {}
+
+        def widen(key, src, sc, vector=()):
+            w_ = stage.tile([P, J, W], BF16, name="wide", align_bytes=64)
+            wide[key] = w_
+            for j in range(J):
+                v = src[:, j, :].bitcast(FP8)
+                if j in vector:
+                    nc.vector.tensor_scalar(out=w_[:, j, :], in0=v, scalar1=sc[:, j:j + 1], scalar2=None, op0=ALU.mult)
+                else:
+                    nc.scalar.activation(out=w_[:, j, :], in_=v, func=ACT.Copy, scale=sc[:, j:j + 1])
+
+        def widen_a(c, g, vector=()):
+            widen(("a", c, g), wgb[c, g], wgs[:, c, :], vector)
+
+        def widen_d(g, h, vector=()):
+            widen(("d", g, h), wdb[g][:, :, h * W:(h + 1) * W], wds[:, g, :], vector)
+
+        def inter(kind, c, g, scalar=False):
+            key = (kind, c, g)
+            src = wur[c, g] if kind == "u" else wide[key][:]
+            g_ = stage.tile([P, W * J], BF16, name="grp", align_bytes=64)
+            grp[key] = g_
+            if kind == "d":
+                o_ = g_[:].rearrange("p (c i j) -> p c j i", i=4, j=J)
+                i_ = src.rearrange("p j (c i) -> p c j i", i=4)
+            else:
+                o_ = g_[:].rearrange("p (t m j) -> p m j t", t=J, j=J)
+                i_ = src.rearrange("p j (m t) -> p m j t", t=J)
+            if scalar:
+                nc.scalar.copy(out=o_, in_=i_)
+            else:
+                nc.vector.tensor_copy(out=o_, in_=i_)
+
+        def quant(kind, c, g):
+            key = (kind, c, g)
+            q_ = keep.tile([P, W], U32, name="q_%s_%d_%d" % key, align_bytes=64)
+            s_ = keep.tile([P, W], U8, name="s_%s_%d_%d" % key, align_bytes=64)
+            nc.vector.quantize_mx(out=q_[:].bitcast(FP8X4), scales=s_[:], in_=grp[key][:])
+            codes[key] = q_
+            scales[key] = s_
+
+        xg = {}
+        xps = {}
+
+        def x_turn(b):
+            bank = psum.tile([P, NC * 2, P], F32, name="bank")
+            words = xs[b][:].bitcast(F32)
+            for c in range(NC):
+                for u in range(2):
+                    nc.tensor.transpose(bank[:, 2 * c + u, :], words[:, 256 * c + u:256 * (c + 1):2], ident[:])
+            xps[b] = bank
+
+        def x_exit(b):
+            if b % 2 == 0:
+                xg[b // 2] = stage.tile([P, NC, TG, J], BF16, name="xg", align_bytes=64)
+            o_ = xg[b // 2][:].rearrange("p c n j -> p c (n j)").bitcast(F32)
+            o_ = o_[:, :, (b % 2) * 256:(b % 2) * 256 + 256].rearrange("p c (r u) -> p c r u", u=2)
+            nc.scalar.copy(out=o_, in_=xps[b][:].rearrange("p (c u) r -> p c r u", u=2))
+
+        def x_quant(tg):
+            q_ = keep.tile([P, NC, TG], U32, name="q_x_%d" % tg, align_bytes=64)
+            s_ = keep.tile([P, NC, TG], U8, name="s_x_%d" % tg, align_bytes=64)
+            nc.vector.quantize_mx(out=q_[:].rearrange("p c n -> p (c n)").bitcast(FP8X4),
+                                  scales=s_[:].rearrange("p c n -> p (c n)"),
+                                  in_=xg[tg][:].rearrange("p c n j -> p (c n j)"))
+            codes["x", tg] = q_
+            scales["x", tg] = s_
+
+        zb = {}
+        ub = {}
+        sg = {}
+        hg = {}
+
+        def mx(o_, lk, lcols, rq, rs, start, stop):
+            nc.tensor.matmul_mx(out=o_, lhsT=codes[lk][:, lcols].bitcast(FP8X4), lhsT_scale=scales[lk][:, lcols],
+                                rhs=rq.bitcast(FP8X4), rhs_scale=rs, start=start, stop=stop)
+
+        def stage1(g, tg):
+            xq, xsc = codes["x", tg], scales["x", tg]
+            for hf in range(2):
+                bank = psum.tile([P, 2, TG], F32, name="bank")
+                for i in range(2):
+                    t = 2 * hf + i
+                    for c in range(NC):
+                        mx(bank[:, i, :], ("a", c, g), slice(t * P, (t + 1) * P), xq[:, c, :], xsc[:, c, :], c == 0, c == NC - 1)
+                zb[hf] = bank
+            for b in range(2):
+                bank = psum.tile([P, J, P], F32, name="bank")
+                cols = slice(b * P, (b + 1) * P)
+                for t in range(J):
+                    for c in range(NC):
+                        mx(bank[:, t, :], ("u", c, g), slice(t * P, (t + 1) * P), xq[:, c, cols], xsc[:, c, cols], c == 0, c == NC - 1)
+                ub[g, tg, b] = bank
+            zb[g, tg] = (zb[0], zb[1])
+
+        def sig(g, tg):
+            s_ = stage.tile([P, J, TG], F32, name="sig")
+            for t in range(J):
+                nc.scalar.activation(out=s_[:, t, :], in_=zb[g, tg][t // 2][:, t % 2, :], func=ACT.Sigmoid, bias=bias[:, g, t:t + 1])
+            sg[g, tg] = s_
+
+        def mul(g, tg):
+            h_ = stage.tile([P, TG, J], BF16, name="hg", align_bytes=64)
+            hg[g, tg] = h_
+            for b in range(2):
+                cols = slice(b * P, (b + 1) * P)
+                nc.vector.tensor_tensor(out=h_[:, cols, :].rearrange("p (c i) t -> p c t i", i=4),
+                                        in0=ub[g, tg, b][:].rearrange("p t (c i) -> p c t i", i=4),
+                                        in1=sg[g, tg][:, :, cols].rearrange("p t (c i) -> p c t i", i=4), op=ALU.mult)
+
+        def hq(g, tg):
+            q_ = keep.tile([P, TG], U32, name="q_h_%d_%d" % (g, tg), align_bytes=64)
+            s_ = keep.tile([P, TG], U8, name="s_h_%d_%d" % (g, tg), align_bytes=64)
+            nc.vector.quantize_mx(out=q_[:].bitcast(FP8X4), scales=s_[:], in_=hg[g, tg][:].rearrange("p n t -> p (n t)"))
+            codes["h", g, tg] = q_
+            scales["h", g, tg] = s_
+
+        yb = {}
+
+        def stage2(h, b, g):
+            if g == 0:
+                yb[h, b] = psum.tile([P, W], F32, name="bank")
+            mx(yb[h, b][:], ("h", g, b // 2), slice((b % 2) * P, (b % 2 + 1) * P), codes["d", g, h][:], scales["d", g, h][:], g == 0, g == NG - 1)
+
+        def leave(h, b):
+            o_ = stage.tile([P, W], F32, name="o", bufs=6)
+            nc.vector.tensor_tensor(out=o_[:], in0=yb[h, b][:], in1=rt[:, b, h * W:(h + 1) * W], op=ALU.add)
+            nc.sync.dma_start(out=out[b * P:(b + 1) * P, h * W:(h + 1) * W], in_=o_[:])
+
+        widen_a(0, 0, vector=(0, 1))
+        x_turn(0)
+        x_turn(1)
+        inter("u", 0, 0)
+        x_exit(0)
+        x_exit(1)
+        inter("a", 0, 0)
+        widen_a(1, 0)
+        quant("u", 0, 0)
+        inter("u", 1, 0)
+        for b in range(2, 6):
+            x_turn(b)
+        quant("a", 0, 0)
+        x_exit(2)
+        x_exit(3)
+        x_quant(0)
+        inter("a", 1, 0)
+        quant("u", 1, 0)
+        x_exit(4)
+        x_exit(5)
+        x_quant(1)
+        quant("a", 1, 0)
+        for g in range(2):
+            n = g + 1
+            stage1(g, 0)
+            widen_a(0, n)
+            inter("u", 0, n)
+            if g == 0:
+                x_quant(2)
+            sig(g, 0)
+            inter("a", 0, n)
+            quant("u", 0, n)
+            stage1(g, 1)
+            widen_a(1, n)
+            mul(g, 0)
+            quant("a", 0, n)
+            hq(g, 0)
+            sig(g, 1)
+            inter("u", 1, n, scalar=True)
+            inter("a", 1, n)
+            mul(g, 1)
+            stage1(g, 2)
+            quant("a", 1, n)
+            hq(g, 1)
+            sig(g, 2)
+            quant("u", 1, n)
+            mul(g, 2)
+            if g == 1:
+                widen_d(0, 0)
+            hq(g, 2)
+        for tg in range(NTG):
+            stage1(2, tg)
+            sig(2, tg)
+            inter("d", tg, 0)
+            if tg < 2:
+                widen_d(tg + 1, 0)
+            mul(2, tg)
+            quant("d", tg, 0)
+            hq(2, tg)
+        for b in range(6):
+            for g in range(NG):
+                stage2(0, b, g)
+        for g in range(NG):
+            widen_d(g, 1)
+            inter("d", g, 1)
+            leave(0, 2 * g)
+            leave(0, 2 * g + 1)
+            quant("d", g, 1)
+            for b in range(6):
+                stage2(1, b, g)
+        for b in range(6):
+            leave(1, b)

@@ -9,12 +9,12 @@ FLOPS = 2 * T * D * F * 2 + 2 * T * F * D
 P = 128
 J = 4
 KP = P * J
-W = 512
 NC = D // KP
 NG = F // KP
-NH = D // W
+W = 512
 TG = 256
-NTG = T // TG
+
+SLICES = ((0, 512), (512, 256), (768, 256))
 
 F32 = mybir.dt.float32
 BF16 = mybir.dt.bfloat16
@@ -34,52 +34,76 @@ def tile_shared_expert_sigmoid_glu_d5_kernel(tc, x, wg_bytes, wg_scale, bg, wu, 
         psum = ctx.enter_context(tc.psum_pool(name="psum", bufs=8))
         ctx.enter_context(tc.manual_schedule())
 
-        wgs = keep.tile([P, NC, 8], F32, name="wgs")
-        nc.scalar.dma_start(out=wgs[:, :, 0:J], in_=wg_scale.rearrange("(c p t) o -> p c (t o)", p=P, t=J))
-        wgb = {}
-        wur = {}
-        xs = {}
-        wdb = {}
-
-        def load_wg(c, lo, n, key):
-            t_ = keep.tile([P, J, n], U8, name="wgb_%d_%d" % (c, lo))
-            nc.sync.dma_start(out=t_[:], in_=wg_bytes[c * KP:(c + 1) * KP, lo:lo + n].rearrange("(p j) n -> p j n", j=J))
-            for g in key:
-                wgb[c, g] = t_[:, :, g * W - lo:(g + 1) * W - lo]
-
-        def load_wu(c, lo, n, key):
-            t_ = keep.tile([P, J, n], BF16, name="wur_%d_%d" % (c, lo))
-            nc.sync.dma_start(out=t_[:], in_=wu[c * KP:(c + 1) * KP, lo:lo + n].rearrange("(p j) n -> p j n", j=J))
-            for g in key:
-                wur[c, g] = t_[:, :, g * W - lo:(g + 1) * W - lo]
-
-        def load_x(b):
-            t_ = keep.tile([P, D], BF16, name="x_%d" % b)
-            nc.sync.dma_start(out=t_[:], in_=x[b * P:(b + 1) * P, :])
-            xs[b] = t_
-
-        load_wg(0, 0, W, (0,))
-        load_wu(0, 0, W, (0,))
-        load_x(0)
-        load_x(1)
-        load_wg(1, 0, W, (0,))
-        load_wu(1, 0, W, (0,))
-        for b in range(2, 6):
-            load_x(b)
-        for c in range(NC):
-            load_wg(c, W, 2 * W, (1, 2))
-            load_wu(c, W, 2 * W, (1, 2))
+        gate_scale = keep.tile([P, NC, 8], F32, name="gate_scale")
+        nc.scalar.dma_start(out=gate_scale[:, :, 0:J], in_=wg_scale.rearrange("(c p j) o -> p c (j o)", p=P, j=J))
         bias = keep.tile([P, NG, J], BF16, name="bias")
         nc.scalar.dma_start(out=bias[:], in_=bg.rearrange("(g p t) -> p g t", p=P, t=J))
-        wds = keep.tile([P, NG, 8], F32, name="wds")
-        nc.scalar.dma_start(out=wds[:, :, 0:J], in_=wd_scale.rearrange("(g p t) o -> p g (t o)", p=P, t=J))
-        for g in range(NG):
-            wdt = keep.tile([P, J, D], U8, name="wdb_%d" % g)
-            nc.sync.dma_start(out=wdt[:], in_=wd_bytes[g * KP:(g + 1) * KP, :].rearrange("(p j) n -> p j n", j=J))
-            wdb[g] = wdt
-        rt = keep.tile([P, T // P, D], BF16, name="rt")
-        for q in range(2):
-            nc.sync.dma_start(out=rt[:, 3 * q:3 * q + 3, :], in_=routed[3 * P * q:3 * P * (q + 1), :].rearrange("(b p) n -> p b n", p=P))
+        down_scale = keep.tile([P, NG, 8], F32, name="down_scale")
+        nc.scalar.dma_start(out=down_scale[:, :, 0:J], in_=wd_scale.rearrange("(g p j) o -> p g (j o)", p=P, j=J))
+
+        gate_bytes = {}
+        up_rows = {}
+        down_bytes = {}
+        x_rows = {}
+        routed_rows = keep.tile([P, T // P, D], BF16, name="routed_rows")
+
+        def load_gate(c, g):
+            src = wg_bytes[c * KP : (c + 1) * KP, g * W : (g + 1) * W].rearrange("(p j) n -> p j n", j=J)
+            if c == 0 and g == 0:
+                planes = []
+                for q in range(2):
+                    half = keep.tile([P, 2, W], U8, name="gate_bytes_0_0_%d" % q)
+                    nc.sync.dma_start(out=half[:], in_=src[:, 2 * q : 2 * q + 2, :])
+                    planes += [half[:, 0, :], half[:, 1, :]]
+            else:
+                whole = keep.tile([P, J, W], U8, name="gate_bytes_%d_%d" % (c, g))
+                nc.sync.dma_start(out=whole[:], in_=src)
+                planes = [whole[:, j, :] for j in range(J)]
+            gate_bytes[c, g] = planes
+
+        def load_up(c, g):
+            rows = keep.tile([P, J, W], BF16, name="up_rows_%d_%d" % (c, g))
+            src = wu[c * KP : (c + 1) * KP, g * W : (g + 1) * W].rearrange("(p j) n -> p j n", j=J)
+            nc.sync.dma_start(out=rows[:], in_=src)
+            up_rows[c, g] = rows
+
+        def load_down(g):
+            rows = keep.tile([P, J, D], U8, name="down_bytes_%d" % g)
+            nc.sync.dma_start(out=rows[:], in_=wd_bytes[g * KP : (g + 1) * KP, :].rearrange("(p j) n -> p j n", j=J))
+            down_bytes[g] = rows
+
+        def load_x(b):
+            rows = keep.tile([P, D], BF16, name="x_rows_%d" % b)
+            nc.sync.dma_start(out=rows[:], in_=x[b * P : (b + 1) * P, :])
+            x_rows[b] = rows
+
+        def load_routed(q):
+            src = routed[3 * P * q : 3 * P * (q + 1), :].rearrange("(b p) n -> p b n", p=P)
+            nc.sync.dma_start(out=routed_rows[:, 3 * q : 3 * q + 3, :], in_=src)
+
+        load_gate(0, 0)
+        load_up(0, 0)
+        load_gate(1, 0)
+        load_up(1, 0)
+        load_up(1, 1)
+        load_gate(1, 1)
+        load_gate(0, 1)
+        load_x(0)
+        load_x(1)
+        load_x(2)
+        load_gate(0, 2)
+        load_x(3)
+        load_up(0, 1)
+        load_gate(1, 2)
+        load_down(0)
+        load_x(4)
+        load_x(5)
+        load_up(1, 2)
+        load_up(0, 2)
+        load_down(1)
+        load_routed(0)
+        load_routed(1)
+        load_down(2)
 
         warm = keep.tile([P, 1], F32, name="warm")
         nc.vector.memset(warm[:], 0.0)
@@ -88,207 +112,307 @@ def tile_shared_expert_sigmoid_glu_d5_kernel(tc, x, wg_bytes, wg_scale, bg, wu, 
         make_identity(nc, ident[:])
 
         wide = {}
-        grp = {}
+        grouped = {}
         codes = {}
         scales = {}
 
-        def widen(key, src, sc, vector=()):
-            w_ = stage.tile([P, J, W], BF16, name="wide", align_bytes=64)
-            wide[key] = w_
+        def columns(key):
+            return SLICES[key[2]][1] if key[0] == "down" else W
+
+        def widen(key, planes, scale, vector):
+            n = columns(key)
+            full = n == W
+            w = stage.tile([P, J, n], BF16, name="wide" if full else "wide_narrow", bufs=4 if full else 3, align_bytes=64)
+            wide[key] = w
             for j in range(J):
-                v = src[:, j, :].bitcast(FP8)
+                values = planes[j].bitcast(FP8)
+                factor = scale[:, j : j + 1]
                 if j in vector:
-                    nc.vector.tensor_scalar(out=w_[:, j, :], in0=v, scalar1=sc[:, j:j + 1], scalar2=None, op0=ALU.mult)
+                    nc.vector.tensor_scalar(out=w[:, j, :], in0=values, scalar1=factor, scalar2=None, op0=ALU.mult)
                 else:
-                    nc.scalar.activation(out=w_[:, j, :], in_=v, func=ACT.Copy, scale=sc[:, j:j + 1])
+                    nc.scalar.activation(out=w[:, j, :], in_=values, func=ACT.Copy, scale=factor)
 
-        def widen_a(c, g, vector=()):
-            widen(("a", c, g), wgb[c, g], wgs[:, c, :], vector)
+        def widen_gate(c, g, vector=()):
+            widen(("gate", c, g), gate_bytes[c, g], gate_scale[:, c, :], vector)
 
-        def widen_d(g, h, vector=()):
-            widen(("d", g, h), wdb[g][:, :, h * W:(h + 1) * W], wds[:, g, :], vector)
+        def widen_down(g, s, vector=()):
+            c0, n = SLICES[s]
+            widen(("down", g, s), [down_bytes[g][:, j, c0 : c0 + n] for j in range(J)], down_scale[:, g, :], vector)
 
-        def inter(kind, c, g, scalar=False):
+        def interleave(kind, c, g, share):
             key = (kind, c, g)
-            src = wur[c, g] if kind == "u" else wide[key][:]
-            g_ = stage.tile([P, W * J], BF16, name="grp", align_bytes=64)
-            grp[key] = g_
-            if kind == "d":
-                o_ = g_[:].rearrange("p (c i j) -> p c j i", i=4, j=J)
-                i_ = src.rearrange("p j (c i) -> p c j i", i=4)
+            n = columns(key)
+            full = n == W
+            dst = stage.tile([P, n * J], BF16, name="grouped" if full else "grouped_narrow", bufs=4 if full else 3, align_bytes=64)
+            grouped[key] = dst
+            src = up_rows[c, g][:] if kind == "up" else wide[key][:]
+            if kind == "down":
+                dst_view = dst[:].rearrange("p (c i j) -> p c j i", i=4, j=J)
+                src_view = src.rearrange("p j (c i) -> p c j i", i=4)
             else:
-                o_ = g_[:].rearrange("p (t m j) -> p m j t", t=J, j=J)
-                i_ = src.rearrange("p j (m t) -> p m j t", t=J)
-            if scalar:
-                nc.scalar.copy(out=o_, in_=i_)
-            else:
-                nc.vector.tensor_copy(out=o_, in_=i_)
+                dst_view = dst[:].rearrange("p (t m r j) -> p m t j r", t=J, r=2, j=J)
+                src_view = src.rearrange("p j (m r t) -> p m t j r", r=2, t=J)
+            steps = dst_view.shape[1]
+            cut = steps - steps * share // 16
+            if cut > 0:
+                nc.vector.tensor_copy(out=dst_view[:, 0:cut], in_=src_view[:, 0:cut])
+            if cut < steps:
+                nc.scalar.copy(out=dst_view[:, cut:steps], in_=src_view[:, cut:steps])
 
-        def quant(kind, c, g):
+        def quantise(kind, c, g):
             key = (kind, c, g)
-            q_ = keep.tile([P, W], U32, name="q_%s_%d_%d" % key, align_bytes=64)
-            s_ = keep.tile([P, W], U8, name="s_%s_%d_%d" % key, align_bytes=64)
-            nc.vector.quantize_mx(out=q_[:].bitcast(FP8X4), scales=s_[:], in_=grp[key][:])
-            codes[key] = q_
-            scales[key] = s_
+            n = columns(key)
+            codes[key] = keep.tile([P, n], U32, name="codes_%s_%d_%d" % key, align_bytes=64)
+            scales[key] = keep.tile([P, n], U8, name="scales_%s_%d_%d" % key, align_bytes=64)
+            nc.vector.quantize_mx(out=codes[key][:].bitcast(FP8X4), scales=scales[key][:], in_=grouped[key][:])
 
-        xg = {}
-        xps = {}
+        x_bank = {}
+        x_grouped = {}
 
-        def x_turn(b):
+        def turn_x(b):
             bank = psum.tile([P, NC * 2, P], F32, name="bank")
-            words = xs[b][:].bitcast(F32)
+            words = x_rows[b][:].bitcast(F32)
             for c in range(NC):
-                for u in range(2):
-                    nc.tensor.transpose(bank[:, 2 * c + u, :], words[:, 256 * c + u:256 * (c + 1):2], ident[:])
-            xps[b] = bank
+                for e in range(2):
+                    nc.tensor.transpose(bank[:, 2 * c + e, :], words[:, 256 * c + e : 256 * (c + 1) : 2], ident[:])
+            x_bank[b] = bank
 
-        def x_exit(b):
+        def copy_x(b):
             if b % 2 == 0:
-                xg[b // 2] = stage.tile([P, NC, TG, J], BF16, name="xg", align_bytes=64)
-            o_ = xg[b // 2][:].rearrange("p c n j -> p c (n j)").bitcast(F32)
-            o_ = o_[:, :, (b % 2) * 256:(b % 2) * 256 + 256].rearrange("p c (r u) -> p c r u", u=2)
-            nc.scalar.copy(out=o_, in_=xps[b][:].rearrange("p (c u) r -> p c r u", u=2))
+                x_grouped[b // 2] = stage.tile([P, NC, TG, J], BF16, name="x_grouped", bufs=3, align_bytes=64)
+            words = x_grouped[b // 2][:].rearrange("p c n j -> p c (n j)").bitcast(F32)
+            dst = words[:, :, (b % 2) * 2 * P : (b % 2 + 1) * 2 * P].rearrange("p c (n e) -> p c n e", e=2)
+            nc.scalar.copy(out=dst, in_=x_bank[b][:].rearrange("p (c e) n -> p c n e", e=2))
 
-        def x_quant(tg):
-            q_ = keep.tile([P, NC, TG], U32, name="q_x_%d" % tg, align_bytes=64)
-            s_ = keep.tile([P, NC, TG], U8, name="s_x_%d" % tg, align_bytes=64)
-            nc.vector.quantize_mx(out=q_[:].rearrange("p c n -> p (c n)").bitcast(FP8X4),
-                                  scales=s_[:].rearrange("p c n -> p (c n)"),
-                                  in_=xg[tg][:].rearrange("p c n j -> p (c n j)"))
-            codes["x", tg] = q_
-            scales["x", tg] = s_
+        def quantise_x(tg):
+            key = ("x", tg)
+            codes[key] = keep.tile([P, NC, TG], U32, name="codes_%s_%d" % key, align_bytes=64)
+            scales[key] = keep.tile([P, NC, TG], U8, name="scales_%s_%d" % key, align_bytes=64)
+            nc.vector.quantize_mx(
+                out=codes[key][:].rearrange("p c n -> p (c n)").bitcast(FP8X4),
+                scales=scales[key][:].rearrange("p c n -> p (c n)"),
+                in_=x_grouped[tg][:].rearrange("p c n j -> p (c n j)"),
+            )
 
-        zb = {}
-        ub = {}
-        sg = {}
-        hg = {}
+        z_banks = {}
+        u_banks = {}
+        gated = {}
+        h_grouped = {}
+        y_bank = {}
 
-        def mx(o_, lk, lcols, rq, rs, start, stop):
-            nc.tensor.matmul_mx(out=o_, lhsT=codes[lk][:, lcols].bitcast(FP8X4), lhsT_scale=scales[lk][:, lcols],
-                                rhs=rq.bitcast(FP8X4), rhs_scale=rs, start=start, stop=stop)
+        def mx(bank, key, cols, rhs, rhs_scale, start, stop):
+            nc.tensor.matmul_mx(
+                out=bank,
+                lhsT=codes[key][:, cols].bitcast(FP8X4),
+                lhsT_scale=scales[key][:, cols],
+                rhs=rhs.bitcast(FP8X4),
+                rhs_scale=rhs_scale,
+                start=start,
+                stop=stop,
+            )
 
-        def stage1(g, tg):
-            xq, xsc = codes["x", tg], scales["x", tg]
-            for hf in range(2):
+        def gate_and_up(g, tg):
+            xq, xs = codes["x", tg], scales["x", tg]
+            z_banks[g, tg] = []
+            for half in range(2):
                 bank = psum.tile([P, 2, TG], F32, name="bank")
                 for i in range(2):
-                    t = 2 * hf + i
+                    t = 2 * half + i
                     for c in range(NC):
-                        mx(bank[:, i, :], ("a", c, g), slice(t * P, (t + 1) * P), xq[:, c, :], xsc[:, c, :], c == 0, c == NC - 1)
-                zb[hf] = bank
+                        mx(bank[:, i, :], ("gate", c, g), slice(t * P, (t + 1) * P), xq[:, c, :], xs[:, c, :], c == 0, c == NC - 1)
+                z_banks[g, tg].append(bank)
+            u_banks[g, tg] = []
             for b in range(2):
                 bank = psum.tile([P, J, P], F32, name="bank")
-                cols = slice(b * P, (b + 1) * P)
+                toks = slice(b * P, (b + 1) * P)
                 for t in range(J):
                     for c in range(NC):
-                        mx(bank[:, t, :], ("u", c, g), slice(t * P, (t + 1) * P), xq[:, c, cols], xsc[:, c, cols], c == 0, c == NC - 1)
-                ub[g, tg, b] = bank
-            zb[g, tg] = (zb[0], zb[1])
+                        mx(bank[:, t, :], ("up", c, g), slice(t * P, (t + 1) * P), xq[:, c, toks], xs[:, c, toks], c == 0, c == NC - 1)
+                u_banks[g, tg].append(bank)
 
-        def sig(g, tg):
-            s_ = stage.tile([P, J, TG], F32, name="sig")
+        def sigmoid(g, tg):
+            s = stage.tile([P, J, TG], F32, name="gated")
             for t in range(J):
-                nc.scalar.activation(out=s_[:, t, :], in_=zb[g, tg][t // 2][:, t % 2, :], func=ACT.Sigmoid, bias=bias[:, g, t:t + 1])
-            sg[g, tg] = s_
+                nc.scalar.activation(out=s[:, t, :], in_=z_banks[g, tg][t // 2][:, t % 2, :], func=ACT.Sigmoid, bias=bias[:, g, t : t + 1])
+            gated[g, tg] = s
 
-        def mul(g, tg):
-            h_ = stage.tile([P, TG, J], BF16, name="hg", align_bytes=64)
-            hg[g, tg] = h_
+        def multiply(g, tg):
+            h = stage.tile([P, TG, J], BF16, name="h_grouped", align_bytes=64)
+            h_grouped[g, tg] = h
             for b in range(2):
-                cols = slice(b * P, (b + 1) * P)
-                nc.vector.tensor_tensor(out=h_[:, cols, :].rearrange("p (c i) t -> p c t i", i=4),
-                                        in0=ub[g, tg, b][:].rearrange("p t (c i) -> p c t i", i=4),
-                                        in1=sg[g, tg][:, :, cols].rearrange("p t (c i) -> p c t i", i=4), op=ALU.mult)
+                toks = slice(b * P, (b + 1) * P)
+                nc.vector.tensor_tensor(
+                    out=h[:, toks, :].rearrange("p (c i) t -> p c t i", i=4),
+                    in0=u_banks[g, tg][b][:].rearrange("p t (c i) -> p c t i", i=4),
+                    in1=gated[g, tg][:, :, toks].rearrange("p t (c i) -> p c t i", i=4),
+                    op=ALU.mult,
+                )
 
-        def hq(g, tg):
-            q_ = keep.tile([P, TG], U32, name="q_h_%d_%d" % (g, tg), align_bytes=64)
-            s_ = keep.tile([P, TG], U8, name="s_h_%d_%d" % (g, tg), align_bytes=64)
-            nc.vector.quantize_mx(out=q_[:].bitcast(FP8X4), scales=s_[:], in_=hg[g, tg][:].rearrange("p n t -> p (n t)"))
-            codes["h", g, tg] = q_
-            scales["h", g, tg] = s_
+        def quantise_h(g, tg):
+            key = ("h", g, tg)
+            codes[key] = keep.tile([P, TG], U32, name="codes_%s_%d_%d" % key, align_bytes=64)
+            scales[key] = keep.tile([P, TG], U8, name="scales_%s_%d_%d" % key, align_bytes=64)
+            nc.vector.quantize_mx(out=codes[key][:].bitcast(FP8X4), scales=scales[key][:], in_=h_grouped[g, tg][:].rearrange("p n t -> p (n t)"))
 
-        yb = {}
-
-        def stage2(h, b, g):
+        def down_pass(s, b, g):
             if g == 0:
-                yb[h, b] = psum.tile([P, W], F32, name="bank")
-            mx(yb[h, b][:], ("h", g, b // 2), slice((b % 2) * P, (b % 2 + 1) * P), codes["d", g, h][:], scales["d", g, h][:], g == 0, g == NG - 1)
+                y_bank[s, b] = psum.tile([P, SLICES[s][1]], F32, name="bank")
+            toks = slice((b % 2) * P, (b % 2 + 1) * P)
+            key = ("down", g, s)
+            mx(y_bank[s, b][:], ("h", g, b // 2), toks, codes[key][:], scales[key][:], g == 0, g == NG - 1)
 
-        def leave(h, b):
-            o_ = stage.tile([P, W], F32, name="o", bufs=6)
-            nc.vector.tensor_tensor(out=o_[:], in0=yb[h, b][:], in1=rt[:, b, h * W:(h + 1) * W], op=ALU.add)
-            nc.sync.dma_start(out=out[b * P:(b + 1) * P, h * W:(h + 1) * W], in_=o_[:])
-
-        widen_a(0, 0, vector=(0, 1))
-        x_turn(0)
-        x_turn(1)
-        inter("u", 0, 0)
-        x_exit(0)
-        x_exit(1)
-        inter("a", 0, 0)
-        widen_a(1, 0)
-        quant("u", 0, 0)
-        inter("u", 1, 0)
-        for b in range(2, 6):
-            x_turn(b)
-        quant("a", 0, 0)
-        x_exit(2)
-        x_exit(3)
-        x_quant(0)
-        inter("a", 1, 0)
-        quant("u", 1, 0)
-        x_exit(4)
-        x_exit(5)
-        x_quant(1)
-        quant("a", 1, 0)
-        for g in range(2):
-            n = g + 1
-            stage1(g, 0)
-            widen_a(0, n)
-            inter("u", 0, n)
-            if g == 0:
-                x_quant(2)
-            sig(g, 0)
-            inter("a", 0, n)
-            quant("u", 0, n)
-            stage1(g, 1)
-            widen_a(1, n)
-            mul(g, 0)
-            quant("a", 0, n)
-            hq(g, 0)
-            sig(g, 1)
-            inter("u", 1, n, scalar=True)
-            inter("a", 1, n)
-            mul(g, 1)
-            stage1(g, 2)
-            quant("a", 1, n)
-            hq(g, 1)
-            sig(g, 2)
-            quant("u", 1, n)
-            mul(g, 2)
-            if g == 1:
-                widen_d(0, 0)
-            hq(g, 2)
-        for tg in range(NTG):
-            stage1(2, tg)
-            sig(2, tg)
-            inter("d", tg, 0)
-            if tg < 2:
-                widen_d(tg + 1, 0)
-            mul(2, tg)
-            quant("d", tg, 0)
-            hq(2, tg)
-        for b in range(6):
+        def down(s, b):
             for g in range(NG):
-                stage2(0, b, g)
-        for g in range(NG):
-            widen_d(g, 1)
-            inter("d", g, 1)
-            leave(0, 2 * g)
-            leave(0, 2 * g + 1)
-            quant("d", g, 1)
-            for b in range(6):
-                stage2(1, b, g)
-        for b in range(6):
-            leave(1, b)
+                down_pass(s, b, g)
+
+        def finish(s, b):
+            c0, n = SLICES[s]
+            full = n == W
+            o = stage.tile([P, n], F32, name="o" if full else "o_narrow", bufs=5 if full else 8)
+            nc.vector.tensor_tensor(out=o[:], in0=y_bank[s, b][:], in1=routed_rows[:, b, c0 : c0 + n], op=ALU.add)
+            nc.sync.dma_start(out=out[b * P : (b + 1) * P, c0 : c0 + n], in_=o[:])
+
+        widen_gate(0, 0, vector=(0, 1, 2))
+        turn_x(0)
+        interleave("gate", 0, 0, share=6)
+        turn_x(1)
+        interleave("up", 0, 0, share=4)
+        quantise("gate", 0, 0)
+        quantise("up", 0, 0)
+        widen_gate(1, 0, vector=(0,))
+        interleave("up", 1, 0, share=6)
+        interleave("gate", 1, 0, share=5)
+        turn_x(2)
+        interleave("up", 1, 1, share=6)
+        widen_gate(1, 1, vector=(0, 1, 2))
+        widen_gate(0, 1)
+        quantise("up", 1, 1)
+        quantise("up", 1, 0)
+        copy_x(0)
+        copy_x(1)
+        quantise("gate", 1, 0)
+        turn_x(3)
+        interleave("gate", 1, 1, share=8)
+        interleave("gate", 0, 1, share=4)
+        quantise_x(0)
+        widen_gate(0, 2, vector=(0, 1, 2, 3))
+        copy_x(2)
+        copy_x(3)
+        quantise("gate", 1, 1)
+
+        gate_and_up(0, 0)
+        interleave("up", 0, 1, share=8)
+        sigmoid(0, 0)
+        turn_x(4)
+        widen_gate(1, 2, vector=(0, 1, 2))
+        quantise_x(1)
+        widen_down(0, 0, vector=(0, 1, 2, 3))
+        gate_and_up(0, 1)
+        widen_down(0, 1)
+        quantise("up", 0, 1)
+        quantise("gate", 0, 1)
+        multiply(0, 0)
+        sigmoid(0, 1)
+        turn_x(5)
+        interleave("up", 1, 2, share=8)
+        copy_x(4)
+        copy_x(5)
+        multiply(0, 1)
+        interleave("up", 0, 2, share=1)
+        gate_and_up(1, 0)
+        quantise_x(2)
+        interleave("gate", 1, 2, share=5)
+        sigmoid(1, 0)
+        gate_and_up(0, 2)
+        interleave("down", 0, 0, share=8)
+        quantise_h(0, 0)
+        quantise("up", 1, 2)
+        sigmoid(0, 2)
+        interleave("gate", 0, 2, share=6)
+        multiply(1, 0)
+        gate_and_up(1, 1)
+        multiply(0, 2)
+        quantise("up", 0, 2)
+        quantise("gate", 1, 2)
+        sigmoid(1, 1)
+        widen_down(1, 0, vector=(0,))
+        interleave("down", 0, 1, share=8)
+        quantise_h(1, 0)
+        quantise_h(0, 1)
+        quantise("gate", 0, 2)
+        gate_and_up(1, 2)
+        quantise_h(0, 2)
+        multiply(1, 1)
+        interleave("down", 1, 0, share=3)
+        widen_down(1, 1, vector=(0,))
+        sigmoid(1, 2)
+
+        gate_and_up(2, 0)
+        sigmoid(2, 0)
+        multiply(1, 2)
+        gate_and_up(2, 1)
+        multiply(2, 0)
+        quantise("down", 0, 1)
+        widen_down(2, 0)
+        widen_down(2, 1, vector=(0, 1, 2))
+        quantise("down", 0, 0)
+        quantise("down", 1, 0)
+        interleave("down", 2, 0, share=6)
+        quantise_h(2, 0)
+        quantise("down", 2, 0)
+        sigmoid(2, 1)
+        multiply(2, 1)
+        gate_and_up(2, 2)
+        quantise_h(1, 1)
+        interleave("down", 1, 1, share=16)
+
+        down(0, 0)
+        quantise_h(1, 2)
+        down(0, 1)
+        quantise_h(2, 1)
+        down(0, 2)
+        sigmoid(2, 2)
+        down(0, 3)
+        multiply(2, 2)
+        quantise("down", 1, 1)
+        interleave("down", 2, 1, share=16)
+        quantise("down", 2, 1)
+        down(1, 0)
+        down(1, 1)
+        finish(0, 0)
+        down(1, 2)
+        widen_down(0, 2)
+        finish(0, 1)
+        finish(0, 2)
+        down(1, 3)
+        quantise_h(2, 2)
+        widen_down(1, 2, vector=(0,))
+        finish(1, 0)
+        interleave("down", 0, 2, share=16)
+        finish(0, 3)
+        quantise("down", 0, 2)
+        down(0, 4)
+        interleave("down", 1, 2, share=16)
+        down(0, 5)
+        finish(1, 1)
+        down(1, 4)
+        finish(0, 4)
+        finish(1, 2)
+        finish(1, 3)
+        down(1, 5)
+        finish(0, 5)
+        widen_down(2, 2)
+        quantise("down", 1, 2)
+        interleave("down", 2, 2, share=8)
+
+        for b in range(T // P):
+            down_pass(2, b, 0)
+        finish(1, 4)
+        quantise("down", 2, 2)
+        finish(1, 5)
+        for b in range(T // P):
+            down_pass(2, b, 1)
+        for b in range(T // P):
+            down_pass(2, b, 2)
+        for b in range(T // P):
+            finish(2, b)

from contextlib import ExitStack

import concourse.mybir as mybir
from concourse.masks import make_identity

T, D, F = 768, 1024, 1536
FLOPS = 2 * T * D * F * 2 + 2 * T * F * D

P = 128
J = 4
KP = P * J
NC = D // KP
NG = F // KP
W = 512
TG = 256

SLICES = ((0, 512), (512, 256), (768, 256))

F32 = mybir.dt.float32
BF16 = mybir.dt.bfloat16
U32 = mybir.dt.uint32
U8 = mybir.dt.uint8
FP8 = mybir.dt.float8_e4m3fn
FP8X4 = mybir.dt.float8_e4m3fn_x4
ACT = mybir.ActivationFunctionType
ALU = mybir.AluOpType


def tile_shared_expert_sigmoid_glu_d5_kernel(tc, x, wg_bytes, wg_scale, bg, wu, wd_bytes, wd_scale, routed, out):
    nc = tc.nc
    with ExitStack() as ctx:
        keep = ctx.enter_context(tc.tile_pool(name="keep", bufs=1))
        stage = ctx.enter_context(tc.tile_pool(name="stage", bufs=4))
        psum = ctx.enter_context(tc.psum_pool(name="psum", bufs=8))
        ctx.enter_context(tc.manual_schedule())

        gate_scale = keep.tile([P, NC, 8], F32, name="gate_scale")
        nc.scalar.dma_start(out=gate_scale[:, :, 0:J], in_=wg_scale.rearrange("(c p j) o -> p c (j o)", p=P, j=J))
        bias = keep.tile([P, NG, J], BF16, name="bias")
        nc.scalar.dma_start(out=bias[:], in_=bg.rearrange("(g p t) -> p g t", p=P, t=J))
        down_scale = keep.tile([P, NG, 8], F32, name="down_scale")
        nc.scalar.dma_start(out=down_scale[:, :, 0:J], in_=wd_scale.rearrange("(g p j) o -> p g (j o)", p=P, j=J))

        gate_bytes = {}
        up_rows = {}
        down_bytes = {}
        x_rows = {}
        routed_rows = keep.tile([P, T // P, D], BF16, name="routed_rows")

        def load_gate(c, g):
            src = wg_bytes[c * KP : (c + 1) * KP, g * W : (g + 1) * W].rearrange("(p j) n -> p j n", j=J)
            if c == 0 and g == 0:
                planes = []
                for q in range(2):
                    half = keep.tile([P, 2, W], U8, name="gate_bytes_0_0_%d" % q)
                    nc.sync.dma_start(out=half[:], in_=src[:, 2 * q : 2 * q + 2, :])
                    planes += [half[:, 0, :], half[:, 1, :]]
            else:
                whole = keep.tile([P, J, W], U8, name="gate_bytes_%d_%d" % (c, g))
                nc.sync.dma_start(out=whole[:], in_=src)
                planes = [whole[:, j, :] for j in range(J)]
            gate_bytes[c, g] = planes

        def load_up(c, g):
            rows = keep.tile([P, J, W], BF16, name="up_rows_%d_%d" % (c, g))
            src = wu[c * KP : (c + 1) * KP, g * W : (g + 1) * W].rearrange("(p j) n -> p j n", j=J)
            nc.sync.dma_start(out=rows[:], in_=src)
            up_rows[c, g] = rows

        def load_down(g):
            rows = keep.tile([P, J, D], U8, name="down_bytes_%d" % g)
            nc.sync.dma_start(out=rows[:], in_=wd_bytes[g * KP : (g + 1) * KP, :].rearrange("(p j) n -> p j n", j=J))
            down_bytes[g] = rows

        def load_x(b):
            rows = keep.tile([P, D], BF16, name="x_rows_%d" % b)
            nc.sync.dma_start(out=rows[:], in_=x[b * P : (b + 1) * P, :])
            x_rows[b] = rows

        def load_routed(q):
            src = routed[3 * P * q : 3 * P * (q + 1), :].rearrange("(b p) n -> p b n", p=P)
            nc.sync.dma_start(out=routed_rows[:, 3 * q : 3 * q + 3, :], in_=src)

        load_gate(0, 0)
        load_up(0, 0)
        load_gate(1, 0)
        load_up(1, 0)
        load_up(1, 1)
        load_gate(1, 1)
        load_gate(0, 1)
        load_x(0)
        load_x(1)
        load_x(2)
        load_gate(0, 2)
        load_x(3)
        load_up(0, 1)
        load_gate(1, 2)
        load_down(0)
        load_x(4)
        load_x(5)
        load_up(1, 2)
        load_up(0, 2)
        load_down(1)
        load_routed(0)
        load_routed(1)
        load_down(2)

        warm = keep.tile([P, 1], F32, name="warm")
        nc.vector.memset(warm[:], 0.0)
        nc.scalar.activation(out=warm[:], in_=warm[:], func=ACT.Sigmoid)
        ident = keep.tile([P, P], F32, name="ident")
        make_identity(nc, ident[:])

        wide = {}
        grouped = {}
        codes = {}
        scales = {}

        def columns(key):
            return SLICES[key[2]][1] if key[0] == "down" else W

        def widen(key, planes, scale, vector):
            n = columns(key)
            full = n == W
            w = stage.tile([P, J, n], BF16, name="wide" if full else "wide_narrow", bufs=4 if full else 3, align_bytes=64)
            wide[key] = w
            for j in range(J):
                values = planes[j].bitcast(FP8)
                factor = scale[:, j : j + 1]
                if j in vector:
                    nc.vector.tensor_scalar(out=w[:, j, :], in0=values, scalar1=factor, scalar2=None, op0=ALU.mult)
                else:
                    nc.scalar.activation(out=w[:, j, :], in_=values, func=ACT.Copy, scale=factor)

        def widen_gate(c, g, vector=()):
            widen(("gate", c, g), gate_bytes[c, g], gate_scale[:, c, :], vector)

        def widen_down(g, s, vector=()):
            c0, n = SLICES[s]
            widen(("down", g, s), [down_bytes[g][:, j, c0 : c0 + n] for j in range(J)], down_scale[:, g, :], vector)

        def interleave(kind, c, g, share):
            key = (kind, c, g)
            n = columns(key)
            full = n == W
            dst = stage.tile([P, n * J], BF16, name="grouped" if full else "grouped_narrow", bufs=4 if full else 3, align_bytes=64)
            grouped[key] = dst
            src = up_rows[c, g][:] if kind == "up" else wide[key][:]
            if kind == "down":
                dst_view = dst[:].rearrange("p (c i j) -> p c j i", i=4, j=J)
                src_view = src.rearrange("p j (c i) -> p c j i", i=4)
            else:
                dst_view = dst[:].rearrange("p (t m r j) -> p m t j r", t=J, r=2, j=J)
                src_view = src.rearrange("p j (m r t) -> p m t j r", r=2, t=J)
            steps = dst_view.shape[1]
            cut = steps - steps * share // 16
            if cut > 0:
                nc.vector.tensor_copy(out=dst_view[:, 0:cut], in_=src_view[:, 0:cut])
            if cut < steps:
                nc.scalar.copy(out=dst_view[:, cut:steps], in_=src_view[:, cut:steps])

        def quantise(kind, c, g):
            key = (kind, c, g)
            n = columns(key)
            codes[key] = keep.tile([P, n], U32, name="codes_%s_%d_%d" % key, align_bytes=64)
            scales[key] = keep.tile([P, n], U8, name="scales_%s_%d_%d" % key, align_bytes=64)
            nc.vector.quantize_mx(out=codes[key][:].bitcast(FP8X4), scales=scales[key][:], in_=grouped[key][:])

        x_bank = {}
        x_grouped = {}

        def turn_x(b):
            bank = psum.tile([P, NC * 2, P], F32, name="bank")
            words = x_rows[b][:].bitcast(F32)
            for c in range(NC):
                for e in range(2):
                    nc.tensor.transpose(bank[:, 2 * c + e, :], words[:, 256 * c + e : 256 * (c + 1) : 2], ident[:])
            x_bank[b] = bank

        def copy_x(b):
            if b % 2 == 0:
                x_grouped[b // 2] = stage.tile([P, NC, TG, J], BF16, name="x_grouped", bufs=3, align_bytes=64)
            words = x_grouped[b // 2][:].rearrange("p c n j -> p c (n j)").bitcast(F32)
            dst = words[:, :, (b % 2) * 2 * P : (b % 2 + 1) * 2 * P].rearrange("p c (n e) -> p c n e", e=2)
            nc.scalar.copy(out=dst, in_=x_bank[b][:].rearrange("p (c e) n -> p c n e", e=2))

        def quantise_x(tg):
            key = ("x", tg)
            codes[key] = keep.tile([P, NC, TG], U32, name="codes_%s_%d" % key, align_bytes=64)
            scales[key] = keep.tile([P, NC, TG], U8, name="scales_%s_%d" % key, align_bytes=64)
            nc.vector.quantize_mx(
                out=codes[key][:].rearrange("p c n -> p (c n)").bitcast(FP8X4),
                scales=scales[key][:].rearrange("p c n -> p (c n)"),
                in_=x_grouped[tg][:].rearrange("p c n j -> p (c n j)"),
            )

        z_banks = {}
        u_banks = {}
        gated = {}
        h_grouped = {}
        y_bank = {}

        def mx(bank, key, cols, rhs, rhs_scale, start, stop):
            nc.tensor.matmul_mx(
                out=bank,
                lhsT=codes[key][:, cols].bitcast(FP8X4),
                lhsT_scale=scales[key][:, cols],
                rhs=rhs.bitcast(FP8X4),
                rhs_scale=rhs_scale,
                start=start,
                stop=stop,
            )

        def gate_and_up(g, tg):
            xq, xs = codes["x", tg], scales["x", tg]
            z_banks[g, tg] = []
            for half in range(2):
                bank = psum.tile([P, 2, TG], F32, name="bank")
                for i in range(2):
                    t = 2 * half + i
                    for c in range(NC):
                        mx(bank[:, i, :], ("gate", c, g), slice(t * P, (t + 1) * P), xq[:, c, :], xs[:, c, :], c == 0, c == NC - 1)
                z_banks[g, tg].append(bank)
            u_banks[g, tg] = []
            for b in range(2):
                bank = psum.tile([P, J, P], F32, name="bank")
                toks = slice(b * P, (b + 1) * P)
                for t in range(J):
                    for c in range(NC):
                        mx(bank[:, t, :], ("up", c, g), slice(t * P, (t + 1) * P), xq[:, c, toks], xs[:, c, toks], c == 0, c == NC - 1)
                u_banks[g, tg].append(bank)

        def sigmoid(g, tg):
            s = stage.tile([P, J, TG], F32, name="gated")
            for t in range(J):
                nc.scalar.activation(out=s[:, t, :], in_=z_banks[g, tg][t // 2][:, t % 2, :], func=ACT.Sigmoid, bias=bias[:, g, t : t + 1])
            gated[g, tg] = s

        def multiply(g, tg):
            h = stage.tile([P, TG, J], BF16, name="h_grouped", align_bytes=64)
            h_grouped[g, tg] = h
            for b in range(2):
                toks = slice(b * P, (b + 1) * P)
                nc.vector.tensor_tensor(
                    out=h[:, toks, :].rearrange("p (c i) t -> p c t i", i=4),
                    in0=u_banks[g, tg][b][:].rearrange("p t (c i) -> p c t i", i=4),
                    in1=gated[g, tg][:, :, toks].rearrange("p t (c i) -> p c t i", i=4),
                    op=ALU.mult,
                )

        def quantise_h(g, tg):
            key = ("h", g, tg)
            codes[key] = keep.tile([P, TG], U32, name="codes_%s_%d_%d" % key, align_bytes=64)
            scales[key] = keep.tile([P, TG], U8, name="scales_%s_%d_%d" % key, align_bytes=64)
            nc.vector.quantize_mx(out=codes[key][:].bitcast(FP8X4), scales=scales[key][:], in_=h_grouped[g, tg][:].rearrange("p n t -> p (n t)"))

        def down_pass(s, b, g):
            if g == 0:
                y_bank[s, b] = psum.tile([P, SLICES[s][1]], F32, name="bank")
            toks = slice((b % 2) * P, (b % 2 + 1) * P)
            key = ("down", g, s)
            mx(y_bank[s, b][:], ("h", g, b // 2), toks, codes[key][:], scales[key][:], g == 0, g == NG - 1)

        def down(s, b):
            for g in range(NG):
                down_pass(s, b, g)

        def finish(s, b):
            c0, n = SLICES[s]
            full = n == W
            o = stage.tile([P, n], F32, name="o" if full else "o_narrow", bufs=5 if full else 8)
            nc.vector.tensor_tensor(out=o[:], in0=y_bank[s, b][:], in1=routed_rows[:, b, c0 : c0 + n], op=ALU.add)
            nc.sync.dma_start(out=out[b * P : (b + 1) * P, c0 : c0 + n], in_=o[:])

        widen_gate(0, 0, vector=(0, 1, 2))
        turn_x(0)
        interleave("gate", 0, 0, share=6)
        turn_x(1)
        interleave("up", 0, 0, share=4)
        quantise("gate", 0, 0)
        quantise("up", 0, 0)
        widen_gate(1, 0, vector=(0,))
        interleave("up", 1, 0, share=6)
        interleave("gate", 1, 0, share=5)
        turn_x(2)
        interleave("up", 1, 1, share=6)
        widen_gate(1, 1, vector=(0, 1, 2))
        widen_gate(0, 1)
        quantise("up", 1, 1)
        quantise("up", 1, 0)
        copy_x(0)
        copy_x(1)
        quantise("gate", 1, 0)
        turn_x(3)
        interleave("gate", 1, 1, share=8)
        interleave("gate", 0, 1, share=4)
        quantise_x(0)
        widen_gate(0, 2, vector=(0, 1, 2, 3))
        copy_x(2)
        copy_x(3)
        quantise("gate", 1, 1)

        gate_and_up(0, 0)
        interleave("up", 0, 1, share=8)
        sigmoid(0, 0)
        turn_x(4)
        widen_gate(1, 2, vector=(0, 1, 2))
        quantise_x(1)
        widen_down(0, 0, vector=(0, 1, 2, 3))
        gate_and_up(0, 1)
        widen_down(0, 1)
        quantise("up", 0, 1)
        quantise("gate", 0, 1)
        multiply(0, 0)
        sigmoid(0, 1)
        turn_x(5)
        interleave("up", 1, 2, share=8)
        copy_x(4)
        copy_x(5)
        multiply(0, 1)
        interleave("up", 0, 2, share=1)
        gate_and_up(1, 0)
        quantise_x(2)
        interleave("gate", 1, 2, share=5)
        sigmoid(1, 0)
        gate_and_up(0, 2)
        interleave("down", 0, 0, share=8)
        quantise_h(0, 0)
        quantise("up", 1, 2)
        sigmoid(0, 2)
        interleave("gate", 0, 2, share=6)
        multiply(1, 0)
        gate_and_up(1, 1)
        multiply(0, 2)
        quantise("up", 0, 2)
        quantise("gate", 1, 2)
        sigmoid(1, 1)
        widen_down(1, 0, vector=(0,))
        interleave("down", 0, 1, share=8)
        quantise_h(1, 0)
        quantise_h(0, 1)
        quantise("gate", 0, 2)
        gate_and_up(1, 2)
        quantise_h(0, 2)
        multiply(1, 1)
        interleave("down", 1, 0, share=3)
        widen_down(1, 1, vector=(0,))
        sigmoid(1, 2)

        gate_and_up(2, 0)
        sigmoid(2, 0)
        multiply(1, 2)
        gate_and_up(2, 1)
        multiply(2, 0)
        quantise("down", 0, 1)
        widen_down(2, 0)
        widen_down(2, 1, vector=(0, 1, 2))
        quantise("down", 0, 0)
        quantise("down", 1, 0)
        interleave("down", 2, 0, share=6)
        quantise_h(2, 0)
        quantise("down", 2, 0)
        sigmoid(2, 1)
        multiply(2, 1)
        gate_and_up(2, 2)
        quantise_h(1, 1)
        interleave("down", 1, 1, share=16)

        down(0, 0)
        quantise_h(1, 2)
        down(0, 1)
        quantise_h(2, 1)
        down(0, 2)
        sigmoid(2, 2)
        down(0, 3)
        multiply(2, 2)
        quantise("down", 1, 1)
        interleave("down", 2, 1, share=16)
        quantise("down", 2, 1)
        down(1, 0)
        down(1, 1)
        finish(0, 0)
        down(1, 2)
        widen_down(0, 2)
        finish(0, 1)
        finish(0, 2)
        down(1, 3)
        quantise_h(2, 2)
        widen_down(1, 2, vector=(0,))
        finish(1, 0)
        interleave("down", 0, 2, share=16)
        finish(0, 3)
        quantise("down", 0, 2)
        down(0, 4)
        interleave("down", 1, 2, share=16)
        down(0, 5)
        finish(1, 1)
        down(1, 4)
        finish(0, 4)
        finish(1, 2)
        finish(1, 3)
        down(1, 5)
        finish(0, 5)
        widen_down(2, 2)
        quantise("down", 1, 2)
        interleave("down", 2, 2, share=8)

        for b in range(T // P):
            down_pass(2, b, 0)
        finish(1, 4)
        quantise("down", 2, 2)
        finish(1, 5)
        for b in range(T // P):
            down_pass(2, b, 1)
        for b in range(T // P):
            down_pass(2, b, 2)
        for b in range(T // P):
            finish(2, b)
